import numpy as np
import ml_dtypes


def mxq(x, axis, fmt="e4m3"):
    dtype, down = {"e4m3": (ml_dtypes.float8_e4m3fn, 7), "e5m2": (ml_dtypes.float8_e5m2, 14)}[fmt]
    v = np.moveaxis(np.asarray(x, np.float32).astype(ml_dtypes.bfloat16).astype(np.float64), axis, -1)
    blocks = v.reshape(v.shape[:-1] + (-1, 32))
    amax = np.abs(blocks).max(-1, keepdims=True)
    byte = np.maximum(np.where(amax > 0, np.frexp(amax)[1] - 1 + 127, 0) - down, 1)
    scale = np.exp2(byte - 127.0)
    codes = (blocks / scale).astype(np.float32).astype(dtype).astype(np.float64)
    return np.moveaxis((codes * scale).reshape(v.shape), -1, axis)


WIDE = False


def mx_kscale(k, group=512):
    if not WIDE:
        return np.ones(k)
    levels = np.array([18, -18])
    if group != 512:
        return np.exp2(np.random.permutation(np.resize(levels, k // group))).repeat(group)
    if k % 512:
        return np.exp2(np.random.permutation(np.resize(levels, k // 32))).repeat(32)
    a = np.empty((k // 512, 16))
    for p in range(k // 512):
        a[p, :8] = np.random.permutation(np.resize(levels, 8))
        for g in range(8):
            far = levels[np.abs(levels - a[p, g]) >= 10]
            a[p, g + 8] = far[np.random.randint(len(far))]
    return np.exp2(a.ravel()).repeat(32)


def f64(x):
    return np.asarray(x).astype(np.float64)


E2M1 = np.array([0.0, 0.5, 1.0, 1.5, 2.0, 3.0, 4.0, 6.0, -0.0, -0.5, -1.0, -1.5, -2.0, -3.0, -4.0, -6.0])


def pack_group(w):
    k, n = w.shape
    w = f64(np.asarray(w, np.float32).astype(ml_dtypes.bfloat16)).reshape(k // 32, 32, n)
    amax = np.abs(w).max(1)
    mant, ex = np.frexp(amax / 6.0)
    byte = np.clip(np.where(amax > 0, np.where(mant > 0.5, ex, ex - 1) + 127, 1), 1, 254)
    scaled = (w * np.exp2(127.0 - byte)[:, None, :]).reshape(k, n).astype(np.float32)
    c = np.ascontiguousarray(scaled.reshape(k // 4, 4, n).transpose(0, 2, 1)).astype(ml_dtypes.float4_e2m1fn).view(np.uint8) & 0xF
    return np.ascontiguousarray((c[..., 0::2] | (c[..., 1::2] << 4)).reshape(k // 4, 2 * n)), byte.astype(np.uint8)


def unpack_group(words, scales):
    p, n = words.shape[0], scales.shape[1]
    words = np.ascontiguousarray(words).reshape(p, n, 2)
    nib = np.empty((p, n, 4), np.uint8)
    nib[..., 0::2] = words & 0xF
    nib[..., 1::2] = words >> 4
    return E2M1[nib].transpose(0, 2, 1).reshape(4 * p, n) * np.repeat(np.exp2(scales.astype(np.float64) - 127.0), 32, axis=0)


G, D, M, N = 4, 128, 128, 512


def setup_inputs():
    n = np.random.standard_normal
    s = mx_kscale(D, 0)[:, None]
    w_ = [pack_group(w) for w in n((G, D, M)) / np.sqrt(D) / s]
    u_ = [pack_group(w) for w in n((G, D, M)) / np.sqrt(D) / s]
    return {
        "x": (n((G, D, N)) * s).astype(np.float32),
        "w_words": np.stack([w[0] for w in w_]),
        "w_scales": np.stack([w[1] for w in w_]),
        "u_words": np.stack([w[0] for w in u_]),
        "u_scales": np.stack([w[1] for w in u_]),
        "b": (0.5 * n((G, M, 1))).astype(np.float32),
        "r": n((G, M, N)).astype(np.float32),
    }


def reference(x, w_words, w_scales, u_words, u_scales, b, r):
    xq = mxq(f64(x), 1, "e4m3")
    h = np.stack([unpack_group(w_words[g], w_scales[g]) for g in range(G)]).transpose(0, 2, 1) @ xq
    g = np.stack([unpack_group(u_words[g], u_scales[g]) for g in range(G)]).transpose(0, 2, 1) @ xq
    h = h + f64(b)
    y = 1.0 / (1.0 + np.exp(-(h))) * g
    y = y + f64(r)
    return y

@@ -1,0 +1,117 @@
+from contextlib import ExitStack
+
+import concourse.mybir as mybir
+
+G, D, M, N = 4, 128, 128, 512
+FLOPS = 2 * 2 * G * D * M * N
+
+F32 = mybir.dt.float32
+BF16 = mybir.dt.bfloat16
+I32 = mybir.dt.int32
+U32 = mybir.dt.uint32
+U8 = mybir.dt.uint8
+FP8X4 = mybir.dt.float8_e4m3fn_x4
+FP4X4 = mybir.dt.float4_e2m1fn_x4
+ALU = mybir.AluOpType
+ACT = mybir.ActivationFunctionType
+
+P = 128
+PACK = 4
+ROWS = D // PACK
+BLOCKS = D // 32
+HALF = N // 2
+VECTOR_COLS = 352
+RUN = 4
+
+
+def tile_rows_gglu_sigmoid_bias_res_kernel(tc, x, w_words, w_scales, u_words, u_scales, b, r, out):
+    nc = tc.nc
+    with ExitStack() as ctx:
+        sb = ctx.enter_context(tc.tile_pool(name="sb", bufs=1))
+        ps = ctx.enter_context(tc.psum_pool(name="ps", bufs=1))
+        ctx.enter_context(tc.manual_schedule())
+
+        x_raw = sb.tile([P, PACK, N], F32, align_bytes=64)
+        x_bf = sb.tile([P, N, PACK], BF16, align_bytes=64)
+        x_codes = sb.tile([P, N], U32, align_bytes=64)
+        x_scale = sb.tile([P, N], U8, align_bytes=64)
+        w_sb = sb.tile([P, 2 * M], U8, align_bytes=64)
+        u_sb = sb.tile([P, 2 * M], U8, align_bytes=64)
+        wu_scale = sb.tile([P, 2 * M], U8, align_bytes=64)
+        b_rows = sb.tile([P, M], F32, align_bytes=64)
+        b_cols = sb.tile([P, M], F32, align_bytes=64)
+        r_sb = [sb.tile([P, 2, N], F32, name=f"r{i}") for i in range(G // 2)]
+
+        nc.vector.memset(wu_scale[:].bitcast(U32), 0)
+        nc.vector.memset(b_rows[:], 0.0)
+
+        nc.scalar.dma_start(out=w_sb[:].bitcast(I32), in_=w_words.rearrange("g p c -> (g p) c").bitcast(I32))
+        nc.sync.dma_start(out=x_raw[:], in_=x.rearrange("g (p j) n -> (g p) j n", j=PACK))
+        nc.scalar.dma_start(out=u_sb[:].bitcast(I32), in_=u_words.rearrange("g p c -> (g p) c").bitcast(I32))
+        nc.scalar.dma_start(
+            out=b_rows[0:P:ROWS, :].rearrange("c (g i) -> c g i", g=G),
+            in_=b.rearrange("g (c i) o -> c g (i o)", i=ROWS),
+        )
+        for g in range(G):
+            live = slice(ROWS * g, ROWS * g + BLOCKS)
+            nc.sync.dma_start(out=wu_scale[live, 0:M].bitcast(I32), in_=w_scales[g].bitcast(I32))
+            nc.gpsimd.dma_start(out=wu_scale[live, M : 2 * M].bitcast(I32), in_=u_scales[g].bitcast(I32))
+        for i in range(G // 2):
+            nc.sync.dma_start(out=r_sb[i][:], in_=r[2 * i : 2 * i + 2].rearrange("g m n -> m g n"))
+
+        def interleave(copy, lo, hi):
+            copy(
+                out=x_bf[:, lo:hi, :].rearrange("p (c i) j -> p c j i", i=RUN),
+                in_=x_raw[:, :, lo:hi].rearrange("p j (c i) -> p c j i", i=RUN),
+            )
+
+        def quantize(lo, hi):
+            nc.vector.quantize_mx(
+                out=x_codes[:, lo:hi].bitcast(FP8X4),
+                scales=x_scale[:, lo:hi],
+                in_=x_bf[:, lo:hi, :].rearrange("p n j -> p (n j)"),
+            )
+
+        interleave(nc.vector.tensor_copy, 0, HALF)
+        interleave(nc.vector.tensor_copy, HALF, VECTOR_COLS)
+        interleave(nc.scalar.copy, VECTOR_COLS, N)
+        quantize(0, HALF)
+        quantize(HALF, N)
+        nc.vector.transpose(out=b_cols[:], in_=b_rows[:])
+
+        def product(acc, words, scale_col, g):
+            rows = slice(ROWS * g, ROWS * (g + 1))
+            nc.tensor.matmul_mx(
+                out=acc[:],
+                lhsT=words[rows, :].bitcast(FP4X4),
+                lhsT_scale=wu_scale[rows, scale_col : scale_col + M],
+                rhs=x_codes[rows, :].bitcast(FP8X4),
+                rhs_scale=x_scale[rows, :],
+                start=True,
+                stop=True,
+            )
+
+        h = [ps.tile([M, N], F32, name=f"h{g}") for g in range(G)]
+        v = [ps.tile([M, N], F32, name=f"v{g}") for g in range(G)]
+        gate = [sb.tile([M, N], F32, name=f"gate{g}") for g in range(G)]
+        gated = [sb.tile([M, N], F32, name=f"gated{g}") for g in range(G)]
+        y = [sb.tile([M, N], F32, name=f"y{g}") for g in range(G)]
+
+        for step in range(G + 1):
+            if step < G:
+                product(h[step], w_sb, 0, step)
+            if step > 0:
+                product(v[step - 1], u_sb, M, step - 1)
+
+        for g in range(G):
+            nc.scalar.activation(
+                out=gate[g][:], in_=h[g][:], func=ACT.Sigmoid, bias=b_cols[:, ROWS * g : ROWS * g + 1]
+            )
+
+        for step in range(G + 1):
+            if step < G:
+                nc.vector.tensor_tensor(out=gated[step][:], in0=v[step][:], in1=gate[step][:], op=ALU.mult)
+            if step > 0:
+                g = step - 1
+                nc.vector.tensor_tensor(out=y[g][:], in0=gated[g][:], in1=r_sb[g // 2][:, g % 2, :], op=ALU.add)
+                nc.sync.dma_start(out=out[g], in_=y[g][:])

@@ -38,7 +38,8 @@ def tile_rows_gglu_sigmoid_bias_res_kernel(tc, x, w_words, w_scales, u_words, u_
         w_sb = sb.tile([P, 2 * M], U8, align_bytes=64)
         u_sb = sb.tile([P, 2 * M], U8, align_bytes=64)
         wu_scale = sb.tile([P, 2 * M], U8, align_bytes=64)
-        b_rows = sb.tile([P, M], F32, align_bytes=64)
+        b_rows = sb.tile([P, M + 8], F32, align_bytes=64)
+        unread = sb.tile([P, 1], F32)
         b_cols = sb.tile([P, M], F32, align_bytes=64)
         r_sb = [sb.tile([P, 2, N], F32, name=f"r{i}") for i in range(G // 2)]
 
@@ -49,9 +50,10 @@ def tile_rows_gglu_sigmoid_bias_res_kernel(tc, x, w_words, w_scales, u_words, u_
         nc.sync.dma_start(out=x_raw[:], in_=x.rearrange("g (p j) n -> (g p) j n", j=PACK))
         nc.scalar.dma_start(out=u_sb[:].bitcast(I32), in_=u_words.rearrange("g p c -> (g p) c").bitcast(I32))
         nc.scalar.dma_start(
-            out=b_rows[0:P:ROWS, :].rearrange("c (g i) -> c g i", g=G),
+            out=b_rows[0:P:ROWS, 0:M].rearrange("c (g i) -> c g i", g=G),
             in_=b.rearrange("g (c i) o -> c g (i o)", i=ROWS),
         )
+        nc.scalar.activation(out=unread[:], in_=b_rows[:, M : M + 1], func=ACT.Sigmoid)
         for g in range(G):
             live = slice(ROWS * g, ROWS * g + BLOCKS)
             nc.sync.dma_start(out=wu_scale[live, 0:M].bitcast(I32), in_=w_scales[g].bitcast(I32))
@@ -77,7 +79,7 @@ def tile_rows_gglu_sigmoid_bias_res_kernel(tc, x, w_words, w_scales, u_words, u_
         interleave(nc.scalar.copy, VECTOR_COLS, N)
         quantize(0, HALF)
         quantize(HALF, N)
-        nc.vector.transpose(out=b_cols[:], in_=b_rows[:])
+        nc.vector.transpose(out=b_cols[:], in_=b_rows[:, 0:M])
 
         def product(acc, words, scale_col, g):
             rows = slice(ROWS * g, ROWS * (g + 1))

@@ -57,7 +57,9 @@ def tile_rows_gglu_sigmoid_bias_res_kernel(tc, x, w_words, w_scales, u_words, u_
         for g in range(G):
             live = slice(ROWS * g, ROWS * g + BLOCKS)
             nc.sync.dma_start(out=wu_scale[live, 0:M].bitcast(I32), in_=w_scales[g].bitcast(I32))
-            nc.gpsimd.dma_start(out=wu_scale[live, M : 2 * M].bitcast(I32), in_=u_scales[g].bitcast(I32))
+        for g in range(G):
+            live = slice(ROWS * g, ROWS * g + BLOCKS)
+            nc.sync.dma_start(out=wu_scale[live, M : 2 * M].bitcast(I32), in_=u_scales[g].bitcast(I32))
         for i in range(G // 2):
             nc.sync.dma_start(out=r_sb[i][:], in_=r[2 * i : 2 * i + 2].rearrange("g m n -> m g n"))
 
@@ -99,21 +101,33 @@ def tile_rows_gglu_sigmoid_bias_res_kernel(tc, x, w_words, w_scales, u_words, u_
         gated = [sb.tile([M, N], F32, name=f"gated{g}") for g in range(G)]
         y = [sb.tile([M, N], F32, name=f"y{g}") for g in range(G)]
 
-        for step in range(G + 1):
-            if step < G:
-                product(h[step], w_sb, 0, step)
-            if step > 0:
-                product(v[step - 1], u_sb, M, step - 1)
+        for g in range(G):
+            product(h[g], w_sb, 0, g)
+        for g in range(G):
+            product(v[g], u_sb, M, g)
 
         for g in range(G):
             nc.scalar.activation(
                 out=gate[g][:], in_=h[g][:], func=ACT.Sigmoid, bias=b_cols[:, ROWS * g : ROWS * g + 1]
             )
 
-        for step in range(G + 1):
-            if step < G:
-                nc.vector.tensor_tensor(out=gated[step][:], in0=v[step][:], in1=gate[step][:], op=ALU.mult)
-            if step > 0:
-                g = step - 1
-                nc.vector.tensor_tensor(out=y[g][:], in0=gated[g][:], in1=r_sb[g // 2][:, g % 2, :], op=ALU.add)
-                nc.sync.dma_start(out=out[g], in_=y[g][:])
+        def multiply(g, cols):
+            nc.vector.tensor_tensor(out=gated[g][:, cols], in0=v[g][:, cols], in1=gate[g][:, cols], op=ALU.mult)
+
+        def add_residual(engine, g, cols):
+            engine.tensor_tensor(out=y[g][:, cols], in0=gated[g][:, cols], in1=r_sb[g // 2][:, g % 2, cols], op=ALU.add)
+
+        left, right, whole = slice(0, HALF), slice(HALF, N), slice(0, N)
+        multiply(0, left)
+        multiply(0, right)
+        for g in range(1, G):
+            multiply(g, whole)
+
+        add_residual(nc.gpsimd, 0, left)
+        add_residual(nc.gpsimd, 0, right)
+        add_residual(nc.gpsimd, 1, left)
+        add_residual(nc.vector, 1, right)
+        for g in range(2, G):
+            add_residual(nc.vector, g, whole)
+        for g in range(G):
+            nc.sync.dma_start(out=out[g], in_=y[g][:])

from contextlib import ExitStack

import concourse.mybir as mybir

G, D, M, N = 4, 128, 128, 512
FLOPS = 2 * 2 * G * D * M * N

F32 = mybir.dt.float32
BF16 = mybir.dt.bfloat16
I32 = mybir.dt.int32
U32 = mybir.dt.uint32
U8 = mybir.dt.uint8
FP8X4 = mybir.dt.float8_e4m3fn_x4
FP4X4 = mybir.dt.float4_e2m1fn_x4
ALU = mybir.AluOpType
ACT = mybir.ActivationFunctionType

P = 128
PACK = 4
ROWS = D // PACK
BLOCKS = D // 32
HALF = N // 2
VECTOR_COLS = 352
RUN = 4


def tile_rows_gglu_sigmoid_bias_res_kernel(tc, x, w_words, w_scales, u_words, u_scales, b, r, out):
    nc = tc.nc
    with ExitStack() as ctx:
        sb = ctx.enter_context(tc.tile_pool(name="sb", bufs=1))
        ps = ctx.enter_context(tc.psum_pool(name="ps", bufs=1))
        ctx.enter_context(tc.manual_schedule())

        x_raw = sb.tile([P, PACK, N], F32, align_bytes=64)
        x_bf = sb.tile([P, N, PACK], BF16, align_bytes=64)
        x_codes = sb.tile([P, N], U32, align_bytes=64)
        x_scale = sb.tile([P, N], U8, align_bytes=64)
        w_sb = sb.tile([P, 2 * M], U8, align_bytes=64)
        u_sb = sb.tile([P, 2 * M], U8, align_bytes=64)
        wu_scale = sb.tile([P, 2 * M], U8, align_bytes=64)
        b_rows = sb.tile([P, M + 8], F32, align_bytes=64)
        unread = sb.tile([P, 1], F32)
        b_cols = sb.tile([P, M], F32, align_bytes=64)
        r_sb = [sb.tile([P, 2, N], F32, name=f"r{i}") for i in range(G // 2)]

        nc.vector.memset(wu_scale[:].bitcast(U32), 0)
        nc.vector.memset(b_rows[:], 0.0)

        nc.scalar.dma_start(out=w_sb[:].bitcast(I32), in_=w_words.rearrange("g p c -> (g p) c").bitcast(I32))
        nc.sync.dma_start(out=x_raw[:], in_=x.rearrange("g (p j) n -> (g p) j n", j=PACK))
        nc.scalar.dma_start(out=u_sb[:].bitcast(I32), in_=u_words.rearrange("g p c -> (g p) c").bitcast(I32))
        nc.scalar.dma_start(
            out=b_rows[0:P:ROWS, 0:M].rearrange("c (g i) -> c g i", g=G),
            in_=b.rearrange("g (c i) o -> c g (i o)", i=ROWS),
        )
        nc.scalar.activation(out=unread[:], in_=b_rows[:, M : M + 1], func=ACT.Sigmoid)
        for g in range(G):
            live = slice(ROWS * g, ROWS * g + BLOCKS)
            nc.sync.dma_start(out=wu_scale[live, 0:M].bitcast(I32), in_=w_scales[g].bitcast(I32))
        for g in range(G):
            live = slice(ROWS * g, ROWS * g + BLOCKS)
            nc.sync.dma_start(out=wu_scale[live, M : 2 * M].bitcast(I32), in_=u_scales[g].bitcast(I32))
        for i in range(G // 2):
            nc.sync.dma_start(out=r_sb[i][:], in_=r[2 * i : 2 * i + 2].rearrange("g m n -> m g n"))

        def interleave(copy, lo, hi):
            copy(
                out=x_bf[:, lo:hi, :].rearrange("p (c i) j -> p c j i", i=RUN),
                in_=x_raw[:, :, lo:hi].rearrange("p j (c i) -> p c j i", i=RUN),
            )

        def quantize(lo, hi):
            nc.vector.quantize_mx(
                out=x_codes[:, lo:hi].bitcast(FP8X4),
                scales=x_scale[:, lo:hi],
                in_=x_bf[:, lo:hi, :].rearrange("p n j -> p (n j)"),
            )

        interleave(nc.vector.tensor_copy, 0, HALF)
        interleave(nc.vector.tensor_copy, HALF, VECTOR_COLS)
        interleave(nc.scalar.copy, VECTOR_COLS, N)
        quantize(0, HALF)
        quantize(HALF, N)
        nc.vector.transpose(out=b_cols[:], in_=b_rows[:, 0:M])

        def product(acc, words, scale_col, g):
            rows = slice(ROWS * g, ROWS * (g + 1))
            nc.tensor.matmul_mx(
                out=acc[:],
                lhsT=words[rows, :].bitcast(FP4X4),
                lhsT_scale=wu_scale[rows, scale_col : scale_col + M],
                rhs=x_codes[rows, :].bitcast(FP8X4),
                rhs_scale=x_scale[rows, :],
                start=True,
                stop=True,
            )

        h = [ps.tile([M, N], F32, name=f"h{g}") for g in range(G)]
        v = [ps.tile([M, N], F32, name=f"v{g}") for g in range(G)]
        gate = [sb.tile([M, N], F32, name=f"gate{g}") for g in range(G)]
        gated = [sb.tile([M, N], F32, name=f"gated{g}") for g in range(G)]
        y = [sb.tile([M, N], F32, name=f"y{g}") for g in range(G)]

        for g in range(G):
            product(h[g], w_sb, 0, g)
        for g in range(G):
            product(v[g], u_sb, M, g)

        for g in range(G):
            nc.scalar.activation(
                out=gate[g][:], in_=h[g][:], func=ACT.Sigmoid, bias=b_cols[:, ROWS * g : ROWS * g + 1]
            )

        def multiply(g, cols):
            nc.vector.tensor_tensor(out=gated[g][:, cols], in0=v[g][:, cols], in1=gate[g][:, cols], op=ALU.mult)

        def add_residual(engine, g, cols):
            engine.tensor_tensor(out=y[g][:, cols], in0=gated[g][:, cols], in1=r_sb[g // 2][:, g % 2, cols], op=ALU.add)

        left, right, whole = slice(0, HALF), slice(HALF, N), slice(0, N)
        multiply(0, left)
        multiply(0, right)
        for g in range(1, G):
            multiply(g, whole)

        add_residual(nc.gpsimd, 0, left)
        add_residual(nc.gpsimd, 0, right)
        add_residual(nc.gpsimd, 1, left)
        add_residual(nc.vector, 1, right)
        for g in range(2, G):
            add_residual(nc.vector, g, whole)
        for g in range(G):
            nc.sync.dma_start(out=out[g], in_=y[g][:])
